import numpy as np
import ml_dtypes


def mxq(x, axis, fmt="e4m3"):
    dtype, down = {"e4m3": (ml_dtypes.float8_e4m3fn, 7), "e5m2": (ml_dtypes.float8_e5m2, 14)}[fmt]
    v = np.moveaxis(np.asarray(x, np.float32).astype(ml_dtypes.bfloat16).astype(np.float64), axis, -1)
    blocks = v.reshape(v.shape[:-1] + (-1, 32))
    amax = np.abs(blocks).max(-1, keepdims=True)
    byte = np.maximum(np.where(amax > 0, np.frexp(amax)[1] - 1 + 127, 0) - down, 1)
    scale = np.exp2(byte - 127.0)
    codes = (blocks / scale).astype(np.float32).astype(dtype).astype(np.float64)
    return np.moveaxis((codes * scale).reshape(v.shape), -1, axis)


WIDE = False


def mx_kscale(k):
    if not WIDE:
        return np.ones(k)
    levels = np.array([10, -10, 5, -5, 0])
    if k % 512:
        return np.exp2(np.random.permutation(np.resize(levels, k // 32))).repeat(32)
    a = np.empty((k // 512, 16))
    for p in range(k // 512):
        a[p, :8] = np.random.permutation(np.resize(levels, 8))
        for g in range(8):
            far = levels[np.abs(levels - a[p, g]) >= 10]
            a[p, g + 8] = far[np.random.randint(len(far))]
    return np.exp2(a.ravel()).repeat(32)


BF16 = ml_dtypes.bfloat16


def bf(x):
    return np.asarray(x, np.float32).astype(BF16)


def f64(x):
    return np.asarray(x).astype(np.float64)


E2M1 = np.array([0.0, 0.5, 1.0, 1.5, 2.0, 3.0, 4.0, 6.0, -0.0, -0.5, -1.0, -1.5, -2.0, -3.0, -4.0, -6.0])


def pack_weight(w, fmt):
    k, n = w.shape
    w = f64(bf(w)).reshape(k // 32, 32, n)
    amax = np.abs(w).max(1)
    if fmt == "e4m3":
        byte = np.frexp(amax)[1] - 1 + 127 - 7
    else:
        mant, ex = np.frexp(amax / 6.0)
        byte = np.where(mant > 0.5, ex, ex - 1) + 127
    byte = np.clip(np.where(amax > 0, byte, 1), 1, 254)
    scaled = (w * np.exp2(127.0 - byte)[:, None, :]).reshape(k, n).astype(np.float32)
    by_word = np.ascontiguousarray(scaled.reshape(k // 512, 128, 4, n).transpose(0, 1, 3, 2))
    if fmt == "e4m3":
        words = by_word.astype(ml_dtypes.float8_e4m3fn).view(np.uint8)
    else:
        c = by_word.astype(ml_dtypes.float4_e2m1fn).view(np.uint8) & 0xF
        words = c[..., 0::2] | (c[..., 1::2] << 4)
    return np.ascontiguousarray(words), np.ascontiguousarray(byte.astype(np.uint8).reshape(k // 512, 16, n))


def unpack_weight(words, scales, fmt):
    g, p, n, _ = words.shape
    if fmt == "e4m3":
        vals = np.ascontiguousarray(words).view(ml_dtypes.float8_e4m3fn).astype(np.float64)
    else:
        nib = np.empty((g, p, n, 4), np.uint8)
        nib[..., 0::2] = words & 0xF
        nib[..., 1::2] = words >> 4
        vals = E2M1[nib]
    vals = vals * np.repeat(np.exp2(scales.astype(np.float64) - 127.0), 8, axis=1)[..., None]
    return vals.transpose(0, 1, 3, 2).reshape(g * 512, n)
def pack4(w):
    words, scales = pack_weight(w, "e2m1")
    return words.reshape(words.shape[0], 128, -1), scales


def unpack4(words, scales):
    return unpack_weight(words.reshape(words.shape[0], 128, -1, 2), scales, "e2m1")


P, C, D, B = 2048, 1024, 1024, 2048


def setup_inputs():
    s, t = mx_kscale(P), mx_kscale(D)
    avg = np.exp(np.random.standard_normal((P, C)) - 1) / np.sqrt(P)
    text = np.random.standard_normal((P, D))
    avg_words, avg_scales = pack4(avg * s[:, None])
    text_words, text_scales = pack4(text / s[:, None] * t)
    return {"avg_words": avg_words, "avg_scales": avg_scales,
            "text_words": text_words, "text_scales": text_scales,
            "gap": bf(0.3 * np.random.standard_normal(D) * t),
            "inv_norm": bf(1 + 0.1 * np.random.standard_normal(C)),
            "images": bf(np.random.standard_normal((B, D)) / np.sqrt(D) / t),
            "prior": bf(0.3 * np.random.standard_normal(C))}


def reference(avg_words, avg_scales, text_words, text_scales, gap, inv_norm, images, prior):
    a = unpack4(avg_words, avg_scales)
    e = unpack4(text_words, text_scales)
    mean = a.T @ e
    cls = (mean + f64(gap)) * f64(inv_norm)[:, None]
    score = mxq(f64(images), 1, "e4m3") @ mxq(cls, 1, "e4m3").T
    return score + f64(prior)

@@ -1,0 +1,294 @@
+from contextlib import ExitStack
+
+import concourse.mybir as mybir
+from concourse.masks import make_identity
+
+PROMPTS, CLASSES, EMBED, IMAGES = 2048, 1024, 1024, 2048
+FLOPS = 2 * CLASSES * EMBED * PROMPTS + 2 * IMAGES * CLASSES * EMBED
+
+F32 = mybir.dt.float32
+BF16 = mybir.dt.bfloat16
+I32 = mybir.dt.int32
+U32 = mybir.dt.uint32
+U8 = mybir.dt.uint8
+FP8X4 = mybir.dt.float8_e4m3fn_x4
+FP4X4 = mybir.dt.float4_e2m1fn_x4
+ADD = mybir.AluOpType.add
+MULT = mybir.AluOpType.mult
+
+P = 128
+PACK = 4
+KG = PROMPTS // 512
+N = 512
+GROUPS = IMAGES // 256
+
+
+def tile_clip_prompt_ensemble_s4_kernel(
+    tc, avg_words, avg_scales, text_words, text_scales, gap, inv_norm, images, prior, out
+):
+    nc = tc.nc
+    with ExitStack() as ctx:
+        keep = ctx.enter_context(tc.tile_pool(name="keep", bufs=1))
+        work = ctx.enter_context(tc.tile_pool(name="work", bufs=2))
+        outs = ctx.enter_context(tc.tile_pool(name="outs", bufs=12))
+        accs = ctx.enter_context(tc.psum_pool(name="accs", bufs=6))
+        turns = ctx.enter_context(tc.psum_pool(name="turns", bufs=2))
+        ctx.enter_context(tc.manual_schedule())
+
+        e_raw = [keep.tile([P, KG, 1024], U8, name="e_raw%d" % h, align_bytes=64) for h in range(2)]
+        e_codes = [keep.tile([P, KG, PACK, 256], U8, name="e_codes%d" % h, align_bytes=64) for h in range(2)]
+        e_scraw = [keep.tile([P, KG, 512], U8, name="e_scraw%d" % h, align_bytes=64) for h in range(2)]
+        e_sc = [keep.tile([P, KG, PACK, 128], U8, name="e_sc%d" % h, align_bytes=64) for h in range(2)]
+        a_codes = [keep.tile([P, KG, 1024], U8, name="a_codes%d" % n, align_bytes=64) for n in range(2)]
+        a_sc = [keep.tile([P, KG, 512], U8, name="a_sc%d" % n, align_bytes=64) for n in range(2)]
+        cls_codes = keep.tile([P, 2, CLASSES], U32, name="cls_codes", align_bytes=64)
+        cls_sc = keep.tile([P, 2, CLASSES], U8, name="cls_sc", align_bytes=64)
+        img_raw = [keep.tile([P, 2, EMBED], BF16, name="img_raw%d" % i, align_bytes=64) for i in range(GROUPS)]
+        img_codes = [keep.tile([P, 2, 256], U32, name="img_codes%d" % i, align_bytes=64) for i in range(GROUPS)]
+        img_sc = [keep.tile([P, 2, 256], U8, name="img_sc%d" % i, align_bytes=64) for i in range(GROUPS)]
+        rows = keep.tile([P, P], BF16, name="rows", align_bytes=64)
+        cols = keep.tile([P, P], BF16, name="cols", align_bytes=64)
+        inv_b = keep.tile([P, CLASSES], BF16, name="inv_b", align_bytes=64)
+        prior_b = keep.tile([P, CLASSES], BF16, name="prior_b", align_bytes=64)
+        gap_sb = keep.tile([P, 2, PACK], BF16, name="gap_sb", align_bytes=64)
+        ident_b = keep.tile([P, P], BF16, name="ident_b", align_bytes=64)
+        ident_f = keep.tile([P, P], F32, name="ident_f", align_bytes=64)
+
+        def zero(engine, t):
+            engine.memset(t[:].rearrange("p g n -> p (g n)").bitcast(I32), 0)
+
+        def load_scales(t, src, half):
+            cs = slice(half * 512, half * 512 + 512)
+            for q in range(4):
+                nc.sync.dma_start(
+                    out=t[32 * q : 32 * q + 4, :, :].bitcast(I32),
+                    in_=src[:, 4 * q : 4 * q + 4, cs].rearrange("g r n -> r g n").bitcast(I32),
+                )
+
+        zero(nc.vector, e_scraw[0])
+        zero(nc.vector, a_sc[0])
+        nc.gpsimd.memset(rows[:], 0.0)
+        load_scales(e_scraw[0], text_scales, 0)
+        load_scales(a_sc[0], avg_scales, 0)
+        nc.scalar.dma_start(out=rows[0:8, :], in_=inv_norm.rearrange("(m n) -> m n", n=P))
+        nc.scalar.dma_start(out=rows[8:16, :], in_=prior.rearrange("(m n) -> m n", n=P))
+        nc.scalar.dma_start(out=gap_sb[:], in_=gap.rearrange("(g p t) -> p g t", p=P, t=PACK))
+        for g in range(KG):
+            nc.sync.dma_start(out=e_raw[0][:, g, :].bitcast(I32), in_=text_words[g, :, 0:1024].bitcast(I32))
+            nc.sync.dma_start(out=a_codes[0][:, g, :].bitcast(I32), in_=avg_words[g, :, 0:1024].bitcast(I32))
+        zero(nc.gpsimd, e_scraw[1])
+        zero(nc.gpsimd, a_sc[1])
+        make_identity(nc, ident_b[:])
+        make_identity(nc, ident_f[:])
+        load_scales(e_scraw[1], text_scales, 1)
+        nc.sync.dma_start(
+            out=e_raw[1][:].bitcast(I32), in_=text_words[:, :, 1024:2048].rearrange("g p n -> p g n").bitcast(I32)
+        )
+        load_scales(a_sc[1], avg_scales, 1)
+        nc.sync.dma_start(
+            out=a_codes[1][:].bitcast(I32), in_=avg_words[:, :, 1024:2048].rearrange("g p n -> p g n").bitcast(I32)
+        )
+        for i in range(GROUPS):
+            nc.sync.dma_start(
+                out=img_raw[i][:], in_=images[256 * i : 256 * i + 256, :].rearrange("(p a) d -> p a d", a=2)
+            )
+
+        colbank = turns.tile([P, P], BF16, name="turn")
+        nc.tensor.transpose(colbank[:], rows[:], ident_b[:])
+        nc.scalar.copy(cols[:], colbank[:])
+        for dst, first in ((inv_b, 0), (prior_b, 8)):
+            spread = turns.tile([P, 8, P], BF16, name="turn")
+            for m in range(8):
+                nc.tensor.transpose(
+                    spread[:, m, :], cols[:, first + m : first + m + 1].to_broadcast([P, P]), ident_b[:]
+                )
+            nc.scalar.copy(dst[:], spread[:].rearrange("p m n -> p (m n)"))
+
+        def perm_codes(h, gs, ts):
+            nc.vector.tensor_copy(
+                out=e_codes[h][:, gs, ts, :].rearrange("p g t (m b) -> p g t m b", b=2),
+                in_=e_raw[h][:, gs, :].rearrange("p g (m t b) -> p g t m b", t=PACK, b=2)[:, :, ts, :, :],
+            )
+
+        def perm_scales(h, gs, ts):
+            nc.vector.tensor_copy(
+                out=e_sc[h][:, gs, ts, :],
+                in_=e_scraw[h][:, gs, :].rearrange("p g (m t) -> p g t m", t=PACK)[:, :, ts, :],
+            )
+
+        def mean_pass(acc, h, n, t, g):
+            nc.tensor.matmul_mx(
+                out=acc[:],
+                lhsT=e_codes[h][:, g, t, :].bitcast(FP4X4),
+                lhsT_scale=e_sc[h][:, g, t, :],
+                rhs=a_codes[n][:, g, :].bitcast(FP4X4),
+                rhs_scale=a_sc[n][:, g, :],
+                start=(g == 0),
+                stop=(g == KG - 1),
+            )
+
+        def stt(acc, raw, h, n, t):
+            nc.vector.scalar_tensor_tensor(
+                out=raw[:, t, :],
+                in0=acc[:],
+                scalar=gap_sb[:, h, t : t + 1],
+                in1=inv_b[:, n * N : n * N + N],
+                op0=ADD,
+                op1=MULT,
+            )
+
+        def interleave(copy, raw):
+            grp = work.tile([P, N, PACK], BF16, name="cls_grp", align_bytes=64)
+            copy(grp[:], raw[:].rearrange("p t c -> p c t"))
+            return grp
+
+        def quant_cls(grp, h, n):
+            ns = slice(n * N, n * N + N)
+            nc.vector.quantize_mx(
+                out=cls_codes[:, h, ns].bitcast(FP8X4),
+                scales=cls_sc[:, h, ns],
+                in_=grp[:].rearrange("p c t -> p (c t)"),
+            )
+
+        def prep(i):
+            words = work.tile([P, 4, 2, P], F32, name="img_words", align_bytes=64)
+            nc.scalar.copy(
+                words[:],
+                img_raw[i][:].rearrange("p a d -> p (a d)").bitcast(F32).rearrange("p (q m u) -> p q u m", q=4, u=2),
+            )
+            return words
+
+        def trans(words):
+            banks = []
+            for g in range(2):
+                bank = turns.tile([P, 2, 2, P], F32, name="turn")
+                for a in range(2):
+                    for u in range(2):
+                        nc.tensor.transpose(bank[:, u, a, :], words[:, 2 * a + g, u, :], ident_f[:])
+                banks.append(bank)
+            return banks
+
+        def evac(banks):
+            grp = work.tile([P, 2, 256, 2], F32, name="img_grp", align_bytes=64)
+            for g in range(2):
+                nc.scalar.copy(grp[:, g, :, :], banks[g][:].rearrange("p u a r -> p (a r) u"))
+            return grp
+
+        def quant_img(grp, i):
+            nc.vector.quantize_mx(
+                out=img_codes[i][:].rearrange("p g r -> p (g r)").bitcast(FP8X4),
+                scales=img_sc[i][:].rearrange("p g r -> p (g r)"),
+                in_=grp[:].rearrange("p g r u -> p (g r u)").bitcast(BF16),
+            )
+
+        out_v = out.rearrange("(i p a) c -> i a p c", p=P, a=2)
+
+        def score(i, a, n):
+            ns = slice(n * N, n * N + N)
+            acc = accs.tile([P, N], F32, name="acc")
+            for g in range(2):
+                nc.tensor.matmul_mx(
+                    out=acc[:],
+                    lhsT=img_codes[i][:, g, a * P : a * P + P].bitcast(FP8X4),
+                    lhsT_scale=img_sc[i][:, g, a * P : a * P + P],
+                    rhs=cls_codes[:, g, ns].bitcast(FP8X4),
+                    rhs_scale=cls_sc[:, g, ns],
+                    start=(g == 0),
+                    stop=(g == 1),
+                )
+            o = outs.tile([P, N], F32, name="o")
+            nc.vector.tensor_tensor(out=o[:], in0=acc[:], in1=prior_b[:, ns], op=ADD)
+            nc.sync.dma_start(out=out_v[i, a, :, ns], in_=o[:])
+
+        acc00 = [accs.tile([P, N], F32, name="acc") for t in range(PACK)]
+        for g in range(KG):
+            perm_scales(0, slice(g, g + 1), slice(0, 4))
+            perm_codes(0, slice(g, g + 1), slice(0, 4))
+            for t in range(PACK):
+                mean_pass(acc00[t], 0, 0, t, g)
+        for t in range(PACK):
+            perm_scales(1, slice(0, 4), slice(t, t + 1))
+            perm_codes(1, slice(0, 4), slice(t, t + 1))
+
+        def unit_t(h, n, t):
+            acc = accs.tile([P, N], F32, name="acc")
+            for g in range(KG):
+                mean_pass(acc, h, n, t, g)
+            return acc
+
+        def raw_tile():
+            raw = work.tile([P, PACK, N], BF16, name="cls_raw", align_bytes=64)
+            return raw
+
+        raw00 = raw_tile()
+        acc10 = []
+        for t in range(PACK):
+            stt(acc00[t], raw00, 0, 0, t)
+            acc10.append(unit_t(1, 0, t))
+        w0 = prep(0)
+        w1 = prep(1)
+        grp00 = interleave(nc.scalar.copy, raw00)
+        raw10 = raw_tile()
+        for t in range(PACK):
+            stt(acc10[t], raw10, 1, 0, t)
+        b0 = trans(w0)
+        i0 = evac(b0)
+        b1 = trans(w1)
+        i1 = evac(b1)
+        grp10 = interleave(nc.vector.tensor_copy, raw10)
+        quant_cls(grp00, 0, 0)
+        quant_cls(grp10, 1, 0)
+        quant_img(i0, 0)
+        w2 = prep(2)
+        w3 = prep(3)
+        raw01 = raw_tile()
+        for t in range(PACK):
+            acc = unit_t(0, 1, t)
+            stt(acc, raw01, 0, 1, t)
+        quant_img(i1, 1)
+        grp01 = interleave(nc.scalar.copy, raw01)
+        b2 = trans(w2)
+        i2 = evac(b2)
+        b3 = trans(w3)
+        i3 = evac(b3)
+        for i in range(2):
+            for a in range(2):
+                score(i, a, 0)
+        quant_cls(grp01, 0, 1)
+        quant_img(i2, 2)
+        quant_img(i3, 3)
+        w4 = prep(4)
+        w5 = prep(5)
+        raw11 = raw_tile()
+        for t in range(PACK):
+            acc = unit_t(1, 1, t)
+            stt(acc, raw11, 1, 1, t)
+        b4 = trans(w4)
+        i4 = evac(b4)
+        b5 = trans(w5)
+        i5 = evac(b5)
+        grp11 = interleave(nc.vector.tensor_copy, raw11)
+        for i in range(2, 4):
+            for a in range(2):
+                score(i, a, 0)
+        quant_cls(grp11, 1, 1)
+        quant_img(i4, 4)
+        quant_img(i5, 5)
+        w6 = prep(6)
+        w7 = prep(7)
+        for i in range(0, 2):
+            for a in range(2):
+                score(i, a, 1)
+        b6 = trans(w6)
+        i6 = evac(b6)
+        b7 = trans(w7)
+        i7 = evac(b7)
+        for i in range(2, 4):
+            for a in range(2):
+                score(i, a, 1)
+        quant_img(i6, 6)
+        quant_img(i7, 7)
+        for i in range(4, 8):
+            for a in range(2):
+                for n in range(2):
+                    score(i, a, n)

@@ -65,38 +65,44 @@ def tile_clip_prompt_ensemble_s4_kernel(
                     in_=src[:, 4 * q : 4 * q + 4, cs].rearrange("g r n -> r g n").bitcast(I32),
                 )
 
-        zero(nc.vector, e_scraw[0])
-        zero(nc.vector, a_sc[0])
-        nc.gpsimd.memset(rows[:], 0.0)
-        load_scales(e_scraw[0], text_scales, 0)
-        load_scales(a_sc[0], avg_scales, 0)
-        nc.scalar.dma_start(out=rows[0:8, :], in_=inv_norm.rearrange("(m n) -> m n", n=P))
-        nc.scalar.dma_start(out=rows[8:16, :], in_=prior.rearrange("(m n) -> m n", n=P))
-        nc.scalar.dma_start(out=gap_sb[:], in_=gap.rearrange("(g p t) -> p g t", p=P, t=PACK))
-        for g in range(KG):
+        def load_text(g):
             nc.sync.dma_start(out=e_raw[0][:, g, :].bitcast(I32), in_=text_words[g, :, 0:1024].bitcast(I32))
             nc.sync.dma_start(out=a_codes[0][:, g, :].bitcast(I32), in_=avg_words[g, :, 0:1024].bitcast(I32))
+
+        zero(nc.vector, e_scraw[0])
+        zero(nc.gpsimd, a_sc[0])
+        nc.gpsimd.memset(rows[:], 0.0)
+        nc.gpsimd.dma_start(out=rows[0:8, :], in_=inv_norm.rearrange("(m n) -> m n", n=P))
+        nc.gpsimd.dma_start(out=rows[8:16, :], in_=prior.rearrange("(m n) -> m n", n=P))
+        nc.gpsimd.dma_start(out=gap_sb[:], in_=gap.rearrange("(g p t) -> p g t", p=P, t=PACK))
+        load_text(0)
+        load_scales(e_scraw[0], text_scales, 0)
+        load_scales(a_sc[0], avg_scales, 0)
+        for g in range(1, KG):
+            load_text(g)
         zero(nc.gpsimd, e_scraw[1])
         zero(nc.gpsimd, a_sc[1])
         make_identity(nc, ident_b[:])
         make_identity(nc, ident_f[:])
-        load_scales(e_scraw[1], text_scales, 1)
         nc.sync.dma_start(
             out=e_raw[1][:].bitcast(I32), in_=text_words[:, :, 1024:2048].rearrange("g p n -> p g n").bitcast(I32)
         )
-        load_scales(a_sc[1], avg_scales, 1)
         nc.sync.dma_start(
             out=a_codes[1][:].bitcast(I32), in_=avg_words[:, :, 1024:2048].rearrange("g p n -> p g n").bitcast(I32)
         )
+        load_scales(e_scraw[1], text_scales, 1)
+        load_scales(a_sc[1], avg_scales, 1)
         for i in range(GROUPS):
             nc.sync.dma_start(
                 out=img_raw[i][:], in_=images[256 * i : 256 * i + 256, :].rearrange("(p a) d -> p a d", a=2)
             )
 
-        colbank = turns.tile([P, P], BF16, name="turn")
-        nc.tensor.transpose(colbank[:], rows[:], ident_b[:])
-        nc.scalar.copy(cols[:], colbank[:])
-        for dst, first in ((inv_b, 0), (prior_b, 8)):
+        def make_columns():
+            colbank = turns.tile([P, P], BF16, name="turn")
+            nc.tensor.transpose(colbank[:], rows[:], ident_b[:])
+            nc.scalar.copy(cols[:], colbank[:])
+
+        def spread_row(dst, first):
             spread = turns.tile([P, 8, P], BF16, name="turn")
             for m in range(8):
                 nc.tensor.transpose(
@@ -137,9 +143,18 @@ def tile_clip_prompt_ensemble_s4_kernel(
                 op1=MULT,
             )
 
-        def interleave(copy, raw):
+        def interleave(raw):
             grp = work.tile([P, N, PACK], BF16, name="cls_grp", align_bytes=64)
-            copy(grp[:], raw[:].rearrange("p t c -> p c t"))
+            half = N // 2
+            nc.scalar.copy(grp[:, :half, :], raw[:, :, :half].rearrange("p t c -> p c t"))
+            nc.gpsimd.tensor_scalar(
+                out=grp[:, half:, :],
+                in0=raw[:, :, half:].rearrange("p t c -> p c t"),
+                scalar1=1.0,
+                scalar2=0.0,
+                op0=MULT,
+                op1=ADD,
+            )
             return grp
 
         def quant_cls(grp, h, n):
@@ -151,7 +166,7 @@ def tile_clip_prompt_ensemble_s4_kernel(
             )
 
         def prep(i):
-            words = work.tile([P, 4, 2, P], F32, name="img_words", align_bytes=64)
+            words = work.tile([P, 4, 2, P], F32, name="img_words", bufs=4, align_bytes=64)
             nc.scalar.copy(
                 words[:],
                 img_raw[i][:].rearrange("p a d -> p (a d)").bitcast(F32).rearrange("p (q m u) -> p q u m", q=4, u=2),
@@ -182,8 +197,14 @@ def tile_clip_prompt_ensemble_s4_kernel(
             )
 
         out_v = out.rearrange("(i p a) c -> i a p c", p=P, a=2)
+        late = []
 
-        def score(i, a, n):
+        def flush(keep_back):
+            while len(late) > keep_back:
+                o, i, a, ns = late.pop(0)
+                nc.sync.dma_start(out=out_v[i, a, :, ns], in_=o[:])
+
+        def score(i, a, n, by_pool=False):
             ns = slice(n * N, n * N + N)
             acc = accs.tile([P, N], F32, name="acc")
             for g in range(2):
@@ -197,8 +218,14 @@ def tile_clip_prompt_ensemble_s4_kernel(
                     stop=(g == 1),
                 )
             o = outs.tile([P, N], F32, name="o")
-            nc.vector.tensor_tensor(out=o[:], in0=acc[:], in1=prior_b[:, ns], op=ADD)
-            nc.sync.dma_start(out=out_v[i, a, :, ns], in_=o[:])
+            if by_pool:
+                s = work.tile([P, N], F32, name="s", align_bytes=64)
+                nc.scalar.copy(s[:], acc[:])
+                nc.gpsimd.tensor_tensor(out=o[:], in0=s[:], in1=prior_b[:, ns], op=ADD)
+                late.append((o, i, a, ns))
+            else:
+                nc.vector.tensor_tensor(out=o[:], in0=acc[:], in1=prior_b[:, ns], op=ADD)
+                nc.sync.dma_start(out=out_v[i, a, :, ns], in_=o[:])
 
         acc00 = [accs.tile([P, N], F32, name="acc") for t in range(PACK)]
         for g in range(KG):
@@ -206,89 +233,66 @@ def tile_clip_prompt_ensemble_s4_kernel(
             perm_codes(0, slice(g, g + 1), slice(0, 4))
             for t in range(PACK):
                 mean_pass(acc00[t], 0, 0, t, g)
+            if g == 2:
+                make_columns()
+        spread_row(inv_b, 0)
+        spread_row(prior_b, 8)
         for t in range(PACK):
-            perm_scales(1, slice(0, 4), slice(t, t + 1))
             perm_codes(1, slice(0, 4), slice(t, t + 1))
+            perm_scales(1, slice(0, 4), slice(t, t + 1))
+
+        raws = {}
+        grps = {}
 
         def unit_t(h, n, t):
             acc = accs.tile([P, N], F32, name="acc")
             for g in range(KG):
                 mean_pass(acc, h, n, t, g)
-            return acc
+            if t == 0:
+                raw = work.tile([P, PACK, N], BF16, name="cls_raw", align_bytes=64)
+                raws[h, n] = raw
+            stt(acc, raws[h, n], h, n, t)
 
-        def raw_tile():
-            raw = work.tile([P, PACK, N], BF16, name="cls_raw", align_bytes=64)
-            return raw
-
-        raw00 = raw_tile()
-        acc10 = []
+        raw00 = work.tile([P, PACK, N], BF16, name="cls_raw", align_bytes=64)
         for t in range(PACK):
             stt(acc00[t], raw00, 0, 0, t)
-            acc10.append(unit_t(1, 0, t))
-        w0 = prep(0)
-        w1 = prep(1)
-        grp00 = interleave(nc.scalar.copy, raw00)
-        raw10 = raw_tile()
-        for t in range(PACK):
-            stt(acc10[t], raw10, 1, 0, t)
-        b0 = trans(w0)
-        i0 = evac(b0)
-        b1 = trans(w1)
-        i1 = evac(b1)
-        grp10 = interleave(nc.vector.tensor_copy, raw10)
-        quant_cls(grp00, 0, 0)
-        quant_cls(grp10, 1, 0)
-        quant_img(i0, 0)
-        w2 = prep(2)
-        w3 = prep(3)
-        raw01 = raw_tile()
-        for t in range(PACK):
-            acc = unit_t(0, 1, t)
-            stt(acc, raw01, 0, 1, t)
-        quant_img(i1, 1)
-        grp01 = interleave(nc.scalar.copy, raw01)
-        b2 = trans(w2)
-        i2 = evac(b2)
-        b3 = trans(w3)
-        i3 = evac(b3)
-        for i in range(2):
-            for a in range(2):
-                score(i, a, 0)
-        quant_cls(grp01, 0, 1)
-        quant_img(i2, 2)
-        quant_img(i3, 3)
-        w4 = prep(4)
-        w5 = prep(5)
-        raw11 = raw_tile()
-        for t in range(PACK):
-            acc = unit_t(1, 1, t)
-            stt(acc, raw11, 1, 1, t)
-        b4 = trans(w4)
-        i4 = evac(b4)
-        b5 = trans(w5)
-        i5 = evac(b5)
-        grp11 = interleave(nc.vector.tensor_copy, raw11)
-        for i in range(2, 4):
-            for a in range(2):
-                score(i, a, 0)
-        quant_cls(grp11, 1, 1)
-        quant_img(i4, 4)
-        quant_img(i5, 5)
-        w6 = prep(6)
-        w7 = prep(7)
-        for i in range(0, 2):
-            for a in range(2):
-                score(i, a, 1)
-        b6 = trans(w6)
-        i6 = evac(b6)
-        b7 = trans(w7)
-        i7 = evac(b7)
-        for i in range(2, 4):
-            for a in range(2):
-                score(i, a, 1)
-        quant_img(i6, 6)
-        quant_img(i7, 7)
-        for i in range(4, 8):
-            for a in range(2):
-                for n in range(2):
-                    score(i, a, n)
+        raws[0, 0] = raw00
+        words = {}
+        words[0] = prep(0)
+        words[1] = prep(1)
+        unit_t(1, 0, 0)
+        unit_t(1, 0, 1)
+        periods = (
+            ("u102", "i00", "u103"),
+            ("u010", "c00", "i10", "u011"),
+            ("u012", "c10", "u013"),
+            ("u110", "i01", "s000", "s010"),
+            ("u111", "c01", "s100", "s110"),
+            ("u112", "s200", "s210"),
+            ("u113", "i11", "s300", "s310"),
+            ("s400", "c11", "s410", "q7", "s500", "s510"),
+        )
+        for i in range(GROUPS):
+            grp = evac(trans(words[i]))
+            for k, task in enumerate(periods[i]):
+                a, b, c = [int(x) for x in ("000" + task[1:])[-3:]]
+                if task[0] == "u":
+                    unit_t(a, b, c)
+                elif task[0] == "i":
+                    grps[b, c] = interleave(raws[b, c])
+                elif task[0] == "c":
+                    quant_cls(grps[b, c], b, c)
+                elif task[0] == "q":
+                    quant_img(grp, i)
+                else:
+                    score(a, b, c)
+            if i + 2 < GROUPS:
+                words[i + 2] = prep(i + 2)
+            if i < GROUPS - 1:
+                quant_img(grp, i)
+        rest = [(6, 0, 0), (6, 1, 0), (7, 0, 0), (7, 1, 0)] + [(i, a, 1) for i in range(GROUPS) for a in range(2)]
+        for k, (i, a, n) in enumerate(rest):
+            score(i, a, n, k % 3 == 1 and k < 17)
+            if k % 3 == 0:
+                flush(0)
+        flush(0)

@@ -31,8 +31,7 @@ def tile_clip_prompt_ensemble_s4_kernel(
         keep = ctx.enter_context(tc.tile_pool(name="keep", bufs=1))
         work = ctx.enter_context(tc.tile_pool(name="work", bufs=2))
         outs = ctx.enter_context(tc.tile_pool(name="outs", bufs=12))
-        accs = ctx.enter_context(tc.psum_pool(name="accs", bufs=6))
-        turns = ctx.enter_context(tc.psum_pool(name="turns", bufs=2))
+        banks = ctx.enter_context(tc.psum_pool(name="banks", bufs=8))
         ctx.enter_context(tc.manual_schedule())
 
         e_raw = [keep.tile([P, KG, 1024], U8, name="e_raw%d" % h, align_bytes=64) for h in range(2)]
@@ -70,40 +69,47 @@ def tile_clip_prompt_ensemble_s4_kernel(
             nc.sync.dma_start(out=a_codes[0][:, g, :].bitcast(I32), in_=avg_words[g, :, 0:1024].bitcast(I32))
 
         zero(nc.vector, e_scraw[0])
-        zero(nc.gpsimd, a_sc[0])
         nc.gpsimd.memset(rows[:], 0.0)
-        nc.gpsimd.dma_start(out=rows[0:8, :], in_=inv_norm.rearrange("(m n) -> m n", n=P))
-        nc.gpsimd.dma_start(out=rows[8:16, :], in_=prior.rearrange("(m n) -> m n", n=P))
-        nc.gpsimd.dma_start(out=gap_sb[:], in_=gap.rearrange("(g p t) -> p g t", p=P, t=PACK))
+        nc.scalar.dma_start(out=rows[0:8, :], in_=inv_norm.rearrange("(m n) -> m n", n=P))
+        make_identity(nc, ident_b[:])
+        zero(nc.vector, a_sc[0])
         load_text(0)
         load_scales(e_scraw[0], text_scales, 0)
         load_scales(a_sc[0], avg_scales, 0)
         for g in range(1, KG):
             load_text(g)
+        make_identity(nc, ident_f[:])
         zero(nc.gpsimd, e_scraw[1])
         zero(nc.gpsimd, a_sc[1])
-        make_identity(nc, ident_b[:])
-        make_identity(nc, ident_f[:])
         nc.sync.dma_start(
             out=e_raw[1][:].bitcast(I32), in_=text_words[:, :, 1024:2048].rearrange("g p n -> p g n").bitcast(I32)
         )
-        nc.sync.dma_start(
-            out=a_codes[1][:].bitcast(I32), in_=avg_words[:, :, 1024:2048].rearrange("g p n -> p g n").bitcast(I32)
-        )
         load_scales(e_scraw[1], text_scales, 1)
         load_scales(a_sc[1], avg_scales, 1)
-        for i in range(GROUPS):
+
+        def load_images(i):
             nc.sync.dma_start(
                 out=img_raw[i][:], in_=images[256 * i : 256 * i + 256, :].rearrange("(p a) d -> p a d", a=2)
             )
 
+        load_images(0)
+        load_images(1)
+        nc.sync.dma_start(
+            out=a_codes[1][:].bitcast(I32), in_=avg_words[:, :, 1024:2048].rearrange("g p n -> p g n").bitcast(I32)
+        )
+        for i in range(2, GROUPS):
+            load_images(i)
+
+        nc.scalar.dma_start(out=gap_sb[:], in_=gap.rearrange("(g p t) -> p g t", p=P, t=PACK))
+        nc.sync.dma_start(out=prior_b[:], in_=prior.partition_broadcast(P))
+
         def make_columns():
-            colbank = turns.tile([P, P], BF16, name="turn")
+            colbank = banks.tile([P, P], BF16, name="bank")
             nc.tensor.transpose(colbank[:], rows[:], ident_b[:])
             nc.scalar.copy(cols[:], colbank[:])
 
         def spread_row(dst, first):
-            spread = turns.tile([P, 8, P], BF16, name="turn")
+            spread = banks.tile([P, 8, P], BF16, name="bank")
             for m in range(8):
                 nc.tensor.transpose(
                     spread[:, m, :], cols[:, first + m : first + m + 1].to_broadcast([P, P]), ident_b[:]
@@ -174,19 +180,19 @@ def tile_clip_prompt_ensemble_s4_kernel(
             return words
 
         def trans(words):
-            banks = []
+            pair = []
             for g in range(2):
-                bank = turns.tile([P, 2, 2, P], F32, name="turn")
+                bank = banks.tile([P, 2, 2, P], F32, name="bank")
                 for a in range(2):
                     for u in range(2):
                         nc.tensor.transpose(bank[:, u, a, :], words[:, 2 * a + g, u, :], ident_f[:])
-                banks.append(bank)
-            return banks
+                pair.append(bank)
+            return pair
 
-        def evac(banks):
+        def evac(pair):
             grp = work.tile([P, 2, 256, 2], F32, name="img_grp", align_bytes=64)
             for g in range(2):
-                nc.scalar.copy(grp[:, g, :, :], banks[g][:].rearrange("p u a r -> p (a r) u"))
+                nc.scalar.copy(grp[:, g, :, :], pair[g][:].rearrange("p u a r -> p (a r) u"))
             return grp
 
         def quant_img(grp, i):
@@ -204,9 +210,9 @@ def tile_clip_prompt_ensemble_s4_kernel(
                 o, i, a, ns = late.pop(0)
                 nc.sync.dma_start(out=out_v[i, a, :, ns], in_=o[:])
 
-        def score(i, a, n, by_pool=False):
+        def multiply(i, a, n):
             ns = slice(n * N, n * N + N)
-            acc = accs.tile([P, N], F32, name="acc")
+            acc = banks.tile([P, N], F32, name="bank")
             for g in range(2):
                 nc.tensor.matmul_mx(
                     out=acc[:],
@@ -217,26 +223,49 @@ def tile_clip_prompt_ensemble_s4_kernel(
                     start=(g == 0),
                     stop=(g == 1),
                 )
-            o = outs.tile([P, N], F32, name="o")
+            return acc
+
+        def score(i, a, n, o, by_pool=False):
+            ns = slice(n * N, n * N + N)
+            acc = multiply(i, a, n)
             if by_pool:
                 s = work.tile([P, N], F32, name="s", align_bytes=64)
                 nc.scalar.copy(s[:], acc[:])
-                nc.gpsimd.tensor_tensor(out=o[:], in0=s[:], in1=prior_b[:, ns], op=ADD)
+                nc.gpsimd.tensor_tensor(out=o, in0=s[:], in1=prior_b[:, ns], op=ADD)
+            else:
+                nc.vector.tensor_tensor(out=o, in0=acc[:], in1=prior_b[:, ns], op=ADD)
+
+        def half_row(i, a, n, by_pool=False):
+            ns = slice(n * N, n * N + N)
+            o = outs.tile([P, N], F32, name="o")
+            score(i, a, n, o[:], by_pool)
+            if by_pool:
                 late.append((o, i, a, ns))
             else:
-                nc.vector.tensor_tensor(out=o[:], in0=acc[:], in1=prior_b[:, ns], op=ADD)
                 nc.sync.dma_start(out=out_v[i, a, :, ns], in_=o[:])
 
-        acc00 = [accs.tile([P, N], F32, name="acc") for t in range(PACK)]
+        def last_half_row(i, a, n):
+            acc = multiply(i, a, n)
+            for c in range(0, N, N // 2):
+                o = outs.tile([P, N // 2], F32, name="o_last", bufs=2)
+                cs = slice(n * N + c, n * N + c + N // 2)
+                nc.vector.tensor_tensor(out=o[:], in0=acc[:, c : c + N // 2], in1=prior_b[:, cs], op=ADD)
+                nc.sync.dma_start(out=out_v[i, a, :, cs], in_=o[:])
+
+        def full_row(i, a):
+            row = outs.tile([P, 2 * N], F32, name="row", bufs=4)
+            score(i, a, 0, row[:, :N])
+            score(i, a, 1, row[:, N:])
+            nc.sync.dma_start(out=out_v[i, a, :, :], in_=row[:])
+
+        make_columns()
+        spread_row(inv_b, 0)
+        acc00 = [banks.tile([P, N], F32, name="bank") for t in range(PACK)]
         for g in range(KG):
             perm_scales(0, slice(g, g + 1), slice(0, 4))
             perm_codes(0, slice(g, g + 1), slice(0, 4))
             for t in range(PACK):
                 mean_pass(acc00[t], 0, 0, t, g)
-            if g == 2:
-                make_columns()
-        spread_row(inv_b, 0)
-        spread_row(prior_b, 8)
         for t in range(PACK):
             perm_codes(1, slice(0, 4), slice(t, t + 1))
             perm_scales(1, slice(0, 4), slice(t, t + 1))
@@ -245,7 +274,7 @@ def tile_clip_prompt_ensemble_s4_kernel(
         grps = {}
 
         def unit_t(h, n, t):
-            acc = accs.tile([P, N], F32, name="acc")
+            acc = banks.tile([P, N], F32, name="bank")
             for g in range(KG):
                 mean_pass(acc, h, n, t, g)
             if t == 0:
@@ -260,39 +289,39 @@ def tile_clip_prompt_ensemble_s4_kernel(
         words = {}
         words[0] = prep(0)
         words[1] = prep(1)
-        unit_t(1, 0, 0)
-        unit_t(1, 0, 1)
-        periods = (
-            ("u102", "i00", "u103"),
-            ("u010", "c00", "i10", "u011"),
-            ("u012", "c10", "u013"),
-            ("u110", "i01", "s000", "s010"),
-            ("u111", "c01", "s100", "s110"),
-            ("u112", "s200", "s210"),
-            ("u113", "i11", "s300", "s310"),
-            ("s400", "c11", "s410", "q7", "s500", "s510"),
+        words[2] = prep(2)
+        for t in range(PACK):
+            unit_t(1, 0, t)
+        steps = (
+            "T00 i00 E00 T01 E01 u010 u011 c00 P03 i10 u012 q00 u013 c10 q01 "
+            "T02 E02 T03 E03 s000 s010 i01 P04 P05 u110 s100 s110 c01 q02 u111 q03 "
+            "T04 E04 T05 E05 s200 P06 u112 s210 s300 q04 u113 i11 P07 s310 q05 s400 s410 c11 s500 s510 "
+            "T06 E06 T07 E07 s001 p011 s101 p111 s201 p211 f q06 s301 q07 p311 s401 p411 f s501 p511 f "
+            "r60 r61 r70 s710 l711 "
         )
-        for i in range(GROUPS):
-            grp = evac(trans(words[i]))
-            for k, task in enumerate(periods[i]):
-                a, b, c = [int(x) for x in ("000" + task[1:])[-3:]]
-                if task[0] == "u":
-                    unit_t(a, b, c)
-                elif task[0] == "i":
-                    grps[b, c] = interleave(raws[b, c])
-                elif task[0] == "c":
-                    quant_cls(grps[b, c], b, c)
-                elif task[0] == "q":
-                    quant_img(grp, i)
-                else:
-                    score(a, b, c)
-            if i + 2 < GROUPS:
-                words[i + 2] = prep(i + 2)
-            if i < GROUPS - 1:
-                quant_img(grp, i)
-        rest = [(6, 0, 0), (6, 1, 0), (7, 0, 0), (7, 1, 0)] + [(i, a, 1) for i in range(GROUPS) for a in range(2)]
-        for k, (i, a, n) in enumerate(rest):
-            score(i, a, n, k % 3 == 1 and k < 17)
-            if k % 3 == 0:
+        grp = {}
+        for step in steps.split():
+            if step == "f":
                 flush(0)
-        flush(0)
+                continue
+            a, b, c = [int(x) for x in ("000" + step[1:])[-3:]]
+            if step[0] == "u":
+                unit_t(a, b, c)
+            elif step[0] == "i":
+                grps[b, c] = interleave(raws[b, c])
+            elif step[0] == "c":
+                quant_cls(grps[b, c], b, c)
+            elif step[0] == "T":
+                grp[c] = trans(words[c])
+            elif step[0] == "E":
+                grp[c] = evac(grp[c])
+            elif step[0] == "P":
+                words[c] = prep(c)
+            elif step[0] == "q":
+                quant_img(grp[c], c)
+            elif step[0] == "r":
+                full_row(b, c)
+            elif step[0] == "l":
+                last_half_row(a, b, c)
+            else:
+                half_row(a, b, c, step[0] == "p")

@@ -71,6 +71,7 @@ def tile_clip_prompt_ensemble_s4_kernel(
         zero(nc.vector, e_scraw[0])
         nc.gpsimd.memset(rows[:], 0.0)
         nc.scalar.dma_start(out=rows[0:8, :], in_=inv_norm.rearrange("(m n) -> m n", n=P))
+        nc.scalar.dma_start(out=rows[8:16, :], in_=prior.rearrange("(m n) -> m n", n=P))
         make_identity(nc, ident_b[:])
         zero(nc.vector, a_sc[0])
         load_text(0)
@@ -78,6 +79,7 @@ def tile_clip_prompt_ensemble_s4_kernel(
         load_scales(a_sc[0], avg_scales, 0)
         for g in range(1, KG):
             load_text(g)
+        nc.sync.dma_start(out=gap_sb[:], in_=gap.rearrange("(g p t) -> p g t", p=P, t=PACK))
         make_identity(nc, ident_f[:])
         zero(nc.gpsimd, e_scraw[1])
         zero(nc.gpsimd, a_sc[1])
@@ -100,8 +102,6 @@ def tile_clip_prompt_ensemble_s4_kernel(
         for i in range(2, GROUPS):
             load_images(i)
 
-        nc.scalar.dma_start(out=gap_sb[:], in_=gap.rearrange("(g p t) -> p g t", p=P, t=PACK))
-        nc.sync.dma_start(out=prior_b[:], in_=prior.partition_broadcast(P))
 
         def make_columns():
             colbank = banks.tile([P, P], BF16, name="bank")
@@ -208,7 +208,7 @@ def tile_clip_prompt_ensemble_s4_kernel(
         def flush(keep_back):
             while len(late) > keep_back:
                 o, i, a, ns = late.pop(0)
-                nc.sync.dma_start(out=out_v[i, a, :, ns], in_=o[:])
+                nc.scalar.dma_start(out=out_v[i, a, :, ns], in_=o[:])
 
         def multiply(i, a, n):
             ns = slice(n * N, n * N + N)
@@ -238,6 +238,8 @@ def tile_clip_prompt_ensemble_s4_kernel(
         def half_row(i, a, n, by_pool=False):
             ns = slice(n * N, n * N + N)
             o = outs.tile([P, N], F32, name="o")
+            if by_pool:
+                flush(0)
             score(i, a, n, o[:], by_pool)
             if by_pool:
                 late.append((o, i, a, ns))
@@ -260,6 +262,18 @@ def tile_clip_prompt_ensemble_s4_kernel(
 
         make_columns()
         spread_row(inv_b, 0)
+        spread_row(prior_b, 8)
+        idle = banks.tile([P, N], F32, name="bank")
+        for k in range(3):
+            nc.tensor.matmul_mx(
+                out=idle[:],
+                lhsT=e_raw[0][:, 0, 0:256].bitcast(FP4X4),
+                lhsT_scale=e_scraw[0][:, 0, 0:128],
+                rhs=a_codes[0][:, 0, :].bitcast(FP4X4),
+                rhs_scale=e_scraw[0][:, 0, :],
+                start=True,
+                stop=True,
+            )
         acc00 = [banks.tile([P, N], F32, name="bank") for t in range(PACK)]
         for g in range(KG):
             perm_scales(0, slice(g, g + 1), slice(0, 4))
@@ -296,8 +310,8 @@ def tile_clip_prompt_ensemble_s4_kernel(
             "T00 i00 E00 T01 E01 u010 u011 c00 P03 i10 u012 q00 u013 c10 q01 "
             "T02 E02 T03 E03 s000 s010 i01 P04 P05 u110 s100 s110 c01 q02 u111 q03 "
             "T04 E04 T05 E05 s200 P06 u112 s210 s300 q04 u113 i11 P07 s310 q05 s400 s410 c11 s500 s510 "
-            "T06 E06 T07 E07 s001 p011 s101 p111 s201 p211 f q06 s301 q07 p311 s401 p411 f s501 p511 f "
-            "r60 r61 r70 s710 l711 "
+            "T06 E06 T07 E07 s001 p011 s101 p111 s201 p211 q06 s301 q07 p311 s401 p411 s501 p511 "
+            "r60 f r61 r70 s710 l711 "
         )
         grp = {}
         for step in steps.split():

@@ -45,12 +45,11 @@ def tile_clip_prompt_ensemble_s4_kernel(
         img_raw = [keep.tile([P, 2, EMBED], BF16, name="img_raw%d" % i, align_bytes=64) for i in range(GROUPS)]
         img_codes = [keep.tile([P, 2, 256], U32, name="img_codes%d" % i, align_bytes=64) for i in range(GROUPS)]
         img_sc = [keep.tile([P, 2, 256], U8, name="img_sc%d" % i, align_bytes=64) for i in range(GROUPS)]
-        rows = keep.tile([P, P], BF16, name="rows", align_bytes=64)
-        cols = keep.tile([P, P], BF16, name="cols", align_bytes=64)
+        rows = keep.tile([P, 2 * P], BF16, name="rows", align_bytes=64)
+        cols = keep.tile([P, P], F32, name="cols", align_bytes=64)
         inv_b = keep.tile([P, CLASSES], BF16, name="inv_b", align_bytes=64)
         prior_b = keep.tile([P, CLASSES], BF16, name="prior_b", align_bytes=64)
         gap_sb = keep.tile([P, 2, PACK], BF16, name="gap_sb", align_bytes=64)
-        ident_b = keep.tile([P, P], BF16, name="ident_b", align_bytes=64)
         ident_f = keep.tile([P, P], F32, name="ident_f", align_bytes=64)
 
         def zero(engine, t):
@@ -70,17 +69,15 @@ def tile_clip_prompt_ensemble_s4_kernel(
 
         zero(nc.vector, e_scraw[0])
         nc.gpsimd.memset(rows[:], 0.0)
-        nc.scalar.dma_start(out=rows[0:8, :], in_=inv_norm.rearrange("(m n) -> m n", n=P))
-        nc.scalar.dma_start(out=rows[8:16, :], in_=prior.rearrange("(m n) -> m n", n=P))
-        make_identity(nc, ident_b[:])
+        nc.scalar.dma_start(out=rows[0:4, :], in_=inv_norm.rearrange("(m n) -> m n", n=2 * P))
+        nc.scalar.dma_start(out=rows[4:8, :], in_=prior.rearrange("(m n) -> m n", n=2 * P))
+        make_identity(nc, ident_f[:])
         zero(nc.vector, a_sc[0])
         load_text(0)
         load_scales(e_scraw[0], text_scales, 0)
         load_scales(a_sc[0], avg_scales, 0)
         for g in range(1, KG):
             load_text(g)
-        nc.sync.dma_start(out=gap_sb[:], in_=gap.rearrange("(g p t) -> p g t", p=P, t=PACK))
-        make_identity(nc, ident_f[:])
         zero(nc.gpsimd, e_scraw[1])
         zero(nc.gpsimd, a_sc[1])
         nc.sync.dma_start(
@@ -94,6 +91,7 @@ def tile_clip_prompt_ensemble_s4_kernel(
                 out=img_raw[i][:], in_=images[256 * i : 256 * i + 256, :].rearrange("(p a) d -> p a d", a=2)
             )
 
+        nc.sync.dma_start(out=gap_sb[:], in_=gap.rearrange("(g p t) -> p g t", p=P, t=PACK))
         load_images(0)
         load_images(1)
         nc.sync.dma_start(
@@ -104,17 +102,17 @@ def tile_clip_prompt_ensemble_s4_kernel(
 
 
         def make_columns():
-            colbank = banks.tile([P, P], BF16, name="bank")
-            nc.tensor.transpose(colbank[:], rows[:], ident_b[:])
-            nc.scalar.copy(cols[:], colbank[:])
+            bank = banks.tile([P, P], F32, name="bank")
+            nc.tensor.transpose(bank[:], rows[:].bitcast(F32), ident_f[:])
+            nc.scalar.copy(cols[:], bank[:])
 
         def spread_row(dst, first):
-            spread = banks.tile([P, 8, P], BF16, name="bank")
-            for m in range(8):
+            bank = banks.tile([P, 4, P], F32, name="bank")
+            for m in range(4):
                 nc.tensor.transpose(
-                    spread[:, m, :], cols[:, first + m : first + m + 1].to_broadcast([P, P]), ident_b[:]
+                    bank[:, m, :], cols[:, first + m : first + m + 1].to_broadcast([P, P]), ident_f[:]
                 )
-            nc.scalar.copy(dst[:], spread[:].rearrange("p m n -> p (m n)"))
+            nc.scalar.copy(dst[:].bitcast(F32), bank[:].rearrange("p m n -> p (m n)"))
 
         def perm_codes(h, gs, ts):
             nc.vector.tensor_copy(
@@ -149,19 +147,16 @@ def tile_clip_prompt_ensemble_s4_kernel(
                 op1=MULT,
             )
 
-        def interleave(raw):
-            grp = work.tile([P, N, PACK], BF16, name="cls_grp", align_bytes=64)
-            half = N // 2
-            nc.scalar.copy(grp[:, :half, :], raw[:, :, :half].rearrange("p t c -> p c t"))
-            nc.gpsimd.tensor_scalar(
-                out=grp[:, half:, :],
-                in0=raw[:, :, half:].rearrange("p t c -> p c t"),
-                scalar1=1.0,
-                scalar2=0.0,
-                op0=MULT,
-                op1=ADD,
-            )
-            return grp
+        def interleave(grp, raw, half, engine):
+            cols = slice(half * (N // 2), (half + 1) * (N // 2))
+            dst = grp[:, cols, :]
+            src = raw[:, :, cols].rearrange("p t c -> p c t")
+            if engine == "i":
+                nc.scalar.copy(dst, src)
+            elif engine == "j":
+                nc.vector.tensor_copy(out=dst, in_=src)
+            else:
+                nc.gpsimd.tensor_scalar(out=dst, in0=src, scalar1=1.0, scalar2=0.0, op0=MULT, op1=ADD)
 
         def quant_cls(grp, h, n):
             ns = slice(n * N, n * N + N)
@@ -208,7 +203,7 @@ def tile_clip_prompt_ensemble_s4_kernel(
         def flush(keep_back):
             while len(late) > keep_back:
                 o, i, a, ns = late.pop(0)
-                nc.scalar.dma_start(out=out_v[i, a, :, ns], in_=o[:])
+                nc.sync.dma_start(out=out_v[i, a, :, ns], in_=o[:])
 
         def multiply(i, a, n):
             ns = slice(n * N, n * N + N)
@@ -238,8 +233,6 @@ def tile_clip_prompt_ensemble_s4_kernel(
         def half_row(i, a, n, by_pool=False):
             ns = slice(n * N, n * N + N)
             o = outs.tile([P, N], F32, name="o")
-            if by_pool:
-                flush(0)
             score(i, a, n, o[:], by_pool)
             if by_pool:
                 late.append((o, i, a, ns))
@@ -262,9 +255,8 @@ def tile_clip_prompt_ensemble_s4_kernel(
 
         make_columns()
         spread_row(inv_b, 0)
-        spread_row(prior_b, 8)
         idle = banks.tile([P, N], F32, name="bank")
-        for k in range(3):
+        for k in range(2):
             nc.tensor.matmul_mx(
                 out=idle[:],
                 lhsT=e_raw[0][:, 0, 0:256].bitcast(FP4X4),
@@ -292,11 +284,11 @@ def tile_clip_prompt_ensemble_s4_kernel(
             for g in range(KG):
                 mean_pass(acc, h, n, t, g)
             if t == 0:
-                raw = work.tile([P, PACK, N], BF16, name="cls_raw", align_bytes=64)
+                raw = work.tile([P, PACK, N], BF16, name="cls_raw", bufs=3, align_bytes=64)
                 raws[h, n] = raw
             stt(acc, raws[h, n], h, n, t)
 
-        raw00 = work.tile([P, PACK, N], BF16, name="cls_raw", align_bytes=64)
+        raw00 = work.tile([P, PACK, N], BF16, name="cls_raw", bufs=3, align_bytes=64)
         for t in range(PACK):
             stt(acc00[t], raw00, 0, 0, t)
         raws[0, 0] = raw00
@@ -307,26 +299,31 @@ def tile_clip_prompt_ensemble_s4_kernel(
         for t in range(PACK):
             unit_t(1, 0, t)
         steps = (
-            "T00 i00 E00 T01 E01 u010 u011 c00 P03 i10 u012 q00 u013 c10 q01 "
-            "T02 E02 T03 E03 s000 s010 i01 P04 P05 u110 s100 s110 c01 q02 u111 q03 "
-            "T04 E04 T05 E05 s200 P06 u112 s210 s300 q04 u113 i11 P07 s310 q05 s400 s410 c11 s500 s510 "
-            "T06 E06 T07 E07 s001 p011 s101 p111 s201 p211 q06 s301 q07 p311 s401 p411 s501 p511 "
-            "r60 f r61 r70 s710 l711 "
+            "u110 T00 P03 j100 u111 E00 T01 j010 u010 u011 E01 B00 q00 P04 g000 T02 g110 c00 c10 u012 u112 "
+            "q01 P05 E02 q02 T03 u013 E03 q03 u113 i001 g101 s000 s010 P06 T04 E04 i011 g111 c01 s100 T05 "
+            "q04 s110 p200 E05 c11 P07 s210 s300 q05 s310 p400 s410 f T06 s001 s011 f E06 s101 s111 q06 s201 "
+            "s211 s301 T07 s311 p401 s411 s500 E07 s501 f s510 q07 s511 s600 s601 s610 s611 s700 s701 s710 "
+            "l711 "
         )
         grp = {}
         for step in steps.split():
-            if step == "f":
-                flush(0)
+            if step[0] == "f":
+                flush(max(0, len(late) - 1))
                 continue
             a, b, c = [int(x) for x in ("000" + step[1:])[-3:]]
             if step[0] == "u":
                 unit_t(a, b, c)
-            elif step[0] == "i":
-                grps[b, c] = interleave(raws[b, c])
+            elif step[0] in "ijg":
+                if (b, c) not in grps:
+                    grouped = work.tile([P, N, PACK], BF16, name="cls_grp", align_bytes=64)
+                    grps[b, c] = grouped
+                interleave(grps[b, c], raws[b, c], a, step[0])
             elif step[0] == "c":
                 quant_cls(grps[b, c], b, c)
             elif step[0] == "T":
                 grp[c] = trans(words[c])
+            elif step[0] == "B":
+                spread_row(prior_b, 4)
             elif step[0] == "E":
                 grp[c] = evac(grp[c])
             elif step[0] == "P":
@@ -339,3 +336,4 @@ def tile_clip_prompt_ensemble_s4_kernel(
                 last_half_row(a, b, c)
             else:
                 half_row(a, b, c, step[0] == "p")
+        flush(0)

from contextlib import ExitStack

import concourse.mybir as mybir
from concourse.masks import make_identity

PROMPTS, CLASSES, EMBED, IMAGES = 2048, 1024, 1024, 2048
FLOPS = 2 * CLASSES * EMBED * PROMPTS + 2 * IMAGES * CLASSES * EMBED

F32 = mybir.dt.float32
BF16 = mybir.dt.bfloat16
I32 = mybir.dt.int32
U32 = mybir.dt.uint32
U8 = mybir.dt.uint8
FP8X4 = mybir.dt.float8_e4m3fn_x4
FP4X4 = mybir.dt.float4_e2m1fn_x4
ADD = mybir.AluOpType.add
MULT = mybir.AluOpType.mult

P = 128
PACK = 4
KG = PROMPTS // 512
N = 512
GROUPS = IMAGES // 256


def tile_clip_prompt_ensemble_s4_kernel(
    tc, avg_words, avg_scales, text_words, text_scales, gap, inv_norm, images, prior, out
):
    nc = tc.nc
    with ExitStack() as ctx:
        keep = ctx.enter_context(tc.tile_pool(name="keep", bufs=1))
        work = ctx.enter_context(tc.tile_pool(name="work", bufs=2))
        outs = ctx.enter_context(tc.tile_pool(name="outs", bufs=12))
        banks = ctx.enter_context(tc.psum_pool(name="banks", bufs=8))
        ctx.enter_context(tc.manual_schedule())

        e_raw = [keep.tile([P, KG, 1024], U8, name="e_raw%d" % h, align_bytes=64) for h in range(2)]
        e_codes = [keep.tile([P, KG, PACK, 256], U8, name="e_codes%d" % h, align_bytes=64) for h in range(2)]
        e_scraw = [keep.tile([P, KG, 512], U8, name="e_scraw%d" % h, align_bytes=64) for h in range(2)]
        e_sc = [keep.tile([P, KG, PACK, 128], U8, name="e_sc%d" % h, align_bytes=64) for h in range(2)]
        a_codes = [keep.tile([P, KG, 1024], U8, name="a_codes%d" % n, align_bytes=64) for n in range(2)]
        a_sc = [keep.tile([P, KG, 512], U8, name="a_sc%d" % n, align_bytes=64) for n in range(2)]
        cls_codes = keep.tile([P, 2, CLASSES], U32, name="cls_codes", align_bytes=64)
        cls_sc = keep.tile([P, 2, CLASSES], U8, name="cls_sc", align_bytes=64)
        img_raw = [keep.tile([P, 2, EMBED], BF16, name="img_raw%d" % i, align_bytes=64) for i in range(GROUPS)]
        img_codes = [keep.tile([P, 2, 256], U32, name="img_codes%d" % i, align_bytes=64) for i in range(GROUPS)]
        img_sc = [keep.tile([P, 2, 256], U8, name="img_sc%d" % i, align_bytes=64) for i in range(GROUPS)]
        rows = keep.tile([P, 2 * P], BF16, name="rows", align_bytes=64)
        cols = keep.tile([P, P], F32, name="cols", align_bytes=64)
        inv_b = keep.tile([P, CLASSES], BF16, name="inv_b", align_bytes=64)
        prior_b = keep.tile([P, CLASSES], BF16, name="prior_b", align_bytes=64)
        gap_sb = keep.tile([P, 2, PACK], BF16, name="gap_sb", align_bytes=64)
        ident_f = keep.tile([P, P], F32, name="ident_f", align_bytes=64)

        def zero(engine, t):
            engine.memset(t[:].rearrange("p g n -> p (g n)").bitcast(I32), 0)

        def load_scales(t, src, half):
            cs = slice(half * 512, half * 512 + 512)
            for q in range(4):
                nc.sync.dma_start(
                    out=t[32 * q : 32 * q + 4, :, :].bitcast(I32),
                    in_=src[:, 4 * q : 4 * q + 4, cs].rearrange("g r n -> r g n").bitcast(I32),
                )

        def load_text(g):
            nc.sync.dma_start(out=e_raw[0][:, g, :].bitcast(I32), in_=text_words[g, :, 0:1024].bitcast(I32))
            nc.sync.dma_start(out=a_codes[0][:, g, :].bitcast(I32), in_=avg_words[g, :, 0:1024].bitcast(I32))

        zero(nc.vector, e_scraw[0])
        nc.gpsimd.memset(rows[:], 0.0)
        nc.scalar.dma_start(out=rows[0:4, :], in_=inv_norm.rearrange("(m n) -> m n", n=2 * P))
        nc.scalar.dma_start(out=rows[4:8, :], in_=prior.rearrange("(m n) -> m n", n=2 * P))
        make_identity(nc, ident_f[:])
        zero(nc.vector, a_sc[0])
        load_text(0)
        load_scales(e_scraw[0], text_scales, 0)
        load_scales(a_sc[0], avg_scales, 0)
        for g in range(1, KG):
            load_text(g)
        zero(nc.gpsimd, e_scraw[1])
        zero(nc.gpsimd, a_sc[1])
        nc.sync.dma_start(
            out=e_raw[1][:].bitcast(I32), in_=text_words[:, :, 1024:2048].rearrange("g p n -> p g n").bitcast(I32)
        )
        load_scales(e_scraw[1], text_scales, 1)
        load_scales(a_sc[1], avg_scales, 1)

        def load_images(i):
            nc.sync.dma_start(
                out=img_raw[i][:], in_=images[256 * i : 256 * i + 256, :].rearrange("(p a) d -> p a d", a=2)
            )

        nc.sync.dma_start(out=gap_sb[:], in_=gap.rearrange("(g p t) -> p g t", p=P, t=PACK))
        load_images(0)
        load_images(1)
        nc.sync.dma_start(
            out=a_codes[1][:].bitcast(I32), in_=avg_words[:, :, 1024:2048].rearrange("g p n -> p g n").bitcast(I32)
        )
        for i in range(2, GROUPS):
            load_images(i)


        def make_columns():
            bank = banks.tile([P, P], F32, name="bank")
            nc.tensor.transpose(bank[:], rows[:].bitcast(F32), ident_f[:])
            nc.scalar.copy(cols[:], bank[:])

        def spread_row(dst, first):
            bank = banks.tile([P, 4, P], F32, name="bank")
            for m in range(4):
                nc.tensor.transpose(
                    bank[:, m, :], cols[:, first + m : first + m + 1].to_broadcast([P, P]), ident_f[:]
                )
            nc.scalar.copy(dst[:].bitcast(F32), bank[:].rearrange("p m n -> p (m n)"))

        def perm_codes(h, gs, ts):
            nc.vector.tensor_copy(
                out=e_codes[h][:, gs, ts, :].rearrange("p g t (m b) -> p g t m b", b=2),
                in_=e_raw[h][:, gs, :].rearrange("p g (m t b) -> p g t m b", t=PACK, b=2)[:, :, ts, :, :],
            )

        def perm_scales(h, gs, ts):
            nc.vector.tensor_copy(
                out=e_sc[h][:, gs, ts, :],
                in_=e_scraw[h][:, gs, :].rearrange("p g (m t) -> p g t m", t=PACK)[:, :, ts, :],
            )

        def mean_pass(acc, h, n, t, g):
            nc.tensor.matmul_mx(
                out=acc[:],
                lhsT=e_codes[h][:, g, t, :].bitcast(FP4X4),
                lhsT_scale=e_sc[h][:, g, t, :],
                rhs=a_codes[n][:, g, :].bitcast(FP4X4),
                rhs_scale=a_sc[n][:, g, :],
                start=(g == 0),
                stop=(g == KG - 1),
            )

        def stt(acc, raw, h, n, t):
            nc.vector.scalar_tensor_tensor(
                out=raw[:, t, :],
                in0=acc[:],
                scalar=gap_sb[:, h, t : t + 1],
                in1=inv_b[:, n * N : n * N + N],
                op0=ADD,
                op1=MULT,
            )

        def interleave(grp, raw, half, engine):
            cols = slice(half * (N // 2), (half + 1) * (N // 2))
            dst = grp[:, cols, :]
            src = raw[:, :, cols].rearrange("p t c -> p c t")
            if engine == "i":
                nc.scalar.copy(dst, src)
            elif engine == "j":
                nc.vector.tensor_copy(out=dst, in_=src)
            else:
                nc.gpsimd.tensor_scalar(out=dst, in0=src, scalar1=1.0, scalar2=0.0, op0=MULT, op1=ADD)

        def quant_cls(grp, h, n):
            ns = slice(n * N, n * N + N)
            nc.vector.quantize_mx(
                out=cls_codes[:, h, ns].bitcast(FP8X4),
                scales=cls_sc[:, h, ns],
                in_=grp[:].rearrange("p c t -> p (c t)"),
            )

        def prep(i):
            words = work.tile([P, 4, 2, P], F32, name="img_words", bufs=4, align_bytes=64)
            nc.scalar.copy(
                words[:],
                img_raw[i][:].rearrange("p a d -> p (a d)").bitcast(F32).rearrange("p (q m u) -> p q u m", q=4, u=2),
            )
            return words

        def trans(words):
            pair = []
            for g in range(2):
                bank = banks.tile([P, 2, 2, P], F32, name="bank")
                for a in range(2):
                    for u in range(2):
                        nc.tensor.transpose(bank[:, u, a, :], words[:, 2 * a + g, u, :], ident_f[:])
                pair.append(bank)
            return pair

        def evac(pair):
            grp = work.tile([P, 2, 256, 2], F32, name="img_grp", align_bytes=64)
            for g in range(2):
                nc.scalar.copy(grp[:, g, :, :], pair[g][:].rearrange("p u a r -> p (a r) u"))
            return grp

        def quant_img(grp, i):
            nc.vector.quantize_mx(
                out=img_codes[i][:].rearrange("p g r -> p (g r)").bitcast(FP8X4),
                scales=img_sc[i][:].rearrange("p g r -> p (g r)"),
                in_=grp[:].rearrange("p g r u -> p (g r u)").bitcast(BF16),
            )

        out_v = out.rearrange("(i p a) c -> i a p c", p=P, a=2)
        late = []

        def flush(keep_back):
            while len(late) > keep_back:
                o, i, a, ns = late.pop(0)
                nc.sync.dma_start(out=out_v[i, a, :, ns], in_=o[:])

        def multiply(i, a, n):
            ns = slice(n * N, n * N + N)
            acc = banks.tile([P, N], F32, name="bank")
            for g in range(2):
                nc.tensor.matmul_mx(
                    out=acc[:],
                    lhsT=img_codes[i][:, g, a * P : a * P + P].bitcast(FP8X4),
                    lhsT_scale=img_sc[i][:, g, a * P : a * P + P],
                    rhs=cls_codes[:, g, ns].bitcast(FP8X4),
                    rhs_scale=cls_sc[:, g, ns],
                    start=(g == 0),
                    stop=(g == 1),
                )
            return acc

        def score(i, a, n, o, by_pool=False):
            ns = slice(n * N, n * N + N)
            acc = multiply(i, a, n)
            if by_pool:
                s = work.tile([P, N], F32, name="s", align_bytes=64)
                nc.scalar.copy(s[:], acc[:])
                nc.gpsimd.tensor_tensor(out=o, in0=s[:], in1=prior_b[:, ns], op=ADD)
            else:
                nc.vector.tensor_tensor(out=o, in0=acc[:], in1=prior_b[:, ns], op=ADD)

        def half_row(i, a, n, by_pool=False):
            ns = slice(n * N, n * N + N)
            o = outs.tile([P, N], F32, name="o")
            score(i, a, n, o[:], by_pool)
            if by_pool:
                late.append((o, i, a, ns))
            else:
                nc.sync.dma_start(out=out_v[i, a, :, ns], in_=o[:])

        def last_half_row(i, a, n):
            acc = multiply(i, a, n)
            for c in range(0, N, N // 2):
                o = outs.tile([P, N // 2], F32, name="o_last", bufs=2)
                cs = slice(n * N + c, n * N + c + N // 2)
                nc.vector.tensor_tensor(out=o[:], in0=acc[:, c : c + N // 2], in1=prior_b[:, cs], op=ADD)
                nc.sync.dma_start(out=out_v[i, a, :, cs], in_=o[:])

        def full_row(i, a):
            row = outs.tile([P, 2 * N], F32, name="row", bufs=4)
            score(i, a, 0, row[:, :N])
            score(i, a, 1, row[:, N:])
            nc.sync.dma_start(out=out_v[i, a, :, :], in_=row[:])

        make_columns()
        spread_row(inv_b, 0)
        idle = banks.tile([P, N], F32, name="bank")
        for k in range(2):
            nc.tensor.matmul_mx(
                out=idle[:],
                lhsT=e_raw[0][:, 0, 0:256].bitcast(FP4X4),
                lhsT_scale=e_scraw[0][:, 0, 0:128],
                rhs=a_codes[0][:, 0, :].bitcast(FP4X4),
                rhs_scale=e_scraw[0][:, 0, :],
                start=True,
                stop=True,
            )
        acc00 = [banks.tile([P, N], F32, name="bank") for t in range(PACK)]
        for g in range(KG):
            perm_scales(0, slice(g, g + 1), slice(0, 4))
            perm_codes(0, slice(g, g + 1), slice(0, 4))
            for t in range(PACK):
                mean_pass(acc00[t], 0, 0, t, g)
        for t in range(PACK):
            perm_codes(1, slice(0, 4), slice(t, t + 1))
            perm_scales(1, slice(0, 4), slice(t, t + 1))

        raws = {}
        grps = {}

        def unit_t(h, n, t):
            acc = banks.tile([P, N], F32, name="bank")
            for g in range(KG):
                mean_pass(acc, h, n, t, g)
            if t == 0:
                raw = work.tile([P, PACK, N], BF16, name="cls_raw", bufs=3, align_bytes=64)
                raws[h, n] = raw
            stt(acc, raws[h, n], h, n, t)

        raw00 = work.tile([P, PACK, N], BF16, name="cls_raw", bufs=3, align_bytes=64)
        for t in range(PACK):
            stt(acc00[t], raw00, 0, 0, t)
        raws[0, 0] = raw00
        words = {}
        words[0] = prep(0)
        words[1] = prep(1)
        words[2] = prep(2)
        for t in range(PACK):
            unit_t(1, 0, t)
        steps = (
            "u110 T00 P03 j100 u111 E00 T01 j010 u010 u011 E01 B00 q00 P04 g000 T02 g110 c00 c10 u012 u112 "
            "q01 P05 E02 q02 T03 u013 E03 q03 u113 i001 g101 s000 s010 P06 T04 E04 i011 g111 c01 s100 T05 "
            "q04 s110 p200 E05 c11 P07 s210 s300 q05 s310 p400 s410 f T06 s001 s011 f E06 s101 s111 q06 s201 "
            "s211 s301 T07 s311 p401 s411 s500 E07 s501 f s510 q07 s511 s600 s601 s610 s611 s700 s701 s710 "
            "l711 "
        )
        grp = {}
        for step in steps.split():
            if step[0] == "f":
                flush(max(0, len(late) - 1))
                continue
            a, b, c = [int(x) for x in ("000" + step[1:])[-3:]]
            if step[0] == "u":
                unit_t(a, b, c)
            elif step[0] in "ijg":
                if (b, c) not in grps:
                    grouped = work.tile([P, N, PACK], BF16, name="cls_grp", align_bytes=64)
                    grps[b, c] = grouped
                interleave(grps[b, c], raws[b, c], a, step[0])
            elif step[0] == "c":
                quant_cls(grps[b, c], b, c)
            elif step[0] == "T":
                grp[c] = trans(words[c])
            elif step[0] == "B":
                spread_row(prior_b, 4)
            elif step[0] == "E":
                grp[c] = evac(grp[c])
            elif step[0] == "P":
                words[c] = prep(c)
            elif step[0] == "q":
                quant_img(grp[c], c)
            elif step[0] == "r":
                full_row(b, c)
            elif step[0] == "l":
                last_half_row(a, b, c)
            else:
                half_row(a, b, c, step[0] == "p")
        flush(0)
